import numpy as np
import ml_dtypes


def mxq(x, axis, fmt="e4m3"):
    dtype, down = {"e4m3": (ml_dtypes.float8_e4m3fn, 7), "e5m2": (ml_dtypes.float8_e5m2, 14)}[fmt]
    v = np.moveaxis(np.asarray(x, np.float32).astype(ml_dtypes.bfloat16).astype(np.float64), axis, -1)
    blocks = v.reshape(v.shape[:-1] + (-1, 32))
    amax = np.abs(blocks).max(-1, keepdims=True)
    byte = np.maximum(np.where(amax > 0, np.frexp(amax)[1] - 1 + 127, 0) - down, 1)
    scale = np.exp2(byte - 127.0)
    codes = (blocks / scale).astype(np.float32).astype(dtype).astype(np.float64)
    return np.moveaxis((codes * scale).reshape(v.shape), -1, axis)


WIDE = False


def mx_kscale(k):
    if not WIDE:
        return np.ones(k)
    levels = np.array([10, -10, 5, -5, 0])
    if k % 512:
        return np.exp2(np.random.permutation(np.resize(levels, k // 32))).repeat(32)
    a = np.empty((k // 512, 16))
    for p in range(k // 512):
        a[p, :8] = np.random.permutation(np.resize(levels, 8))
        for g in range(8):
            far = levels[np.abs(levels - a[p, g]) >= 10]
            a[p, g + 8] = far[np.random.randint(len(far))]
    return np.exp2(a.ravel()).repeat(32)


def f64(x):
    return np.asarray(x).astype(np.float64)


def striped(idx):
    return np.tile(np.asarray(idx).reshape(-1, 16).T, (8, 1)).astype(np.uint16)


def unstriped(offs):
    return offs[:16].T.reshape(-1).astype(np.int64)


E2M1 = np.array([0.0, 0.5, 1.0, 1.5, 2.0, 3.0, 4.0, 6.0, -0.0, -0.5, -1.0, -1.5, -2.0, -3.0, -4.0, -6.0])


def pack_weight(w, fmt):
    k, n = w.shape
    w = f64(np.asarray(w, np.float32).astype(ml_dtypes.bfloat16)).reshape(k // 32, 32, n)
    amax = np.abs(w).max(1)
    if fmt == "e4m3":
        byte = np.frexp(amax)[1] - 1 + 127 - 7
    else:
        mant, ex = np.frexp(amax / 6.0)
        byte = np.where(mant > 0.5, ex, ex - 1) + 127
    byte = np.clip(np.where(amax > 0, byte, 1), 1, 254)
    scaled = (w * np.exp2(127.0 - byte)[:, None, :]).reshape(k, n).astype(np.float32)
    by_word = np.ascontiguousarray(scaled.reshape(k // 512, 128, 4, n).transpose(0, 1, 3, 2))
    if fmt == "e4m3":
        words = by_word.astype(ml_dtypes.float8_e4m3fn).view(np.uint8)
    else:
        c = by_word.astype(ml_dtypes.float4_e2m1fn).view(np.uint8) & 0xF
        words = (c[..., 0::2] | (c[..., 1::2] << 4)).reshape(k // 512, 128, 2 * n)
    return np.ascontiguousarray(words), np.ascontiguousarray(byte.astype(np.uint8).reshape(k // 512, 16, n))


def unpack_weight(words, scales, fmt):
    g, _, n = scales.shape
    words = np.ascontiguousarray(words).reshape(g, 128, n, -1)
    if fmt == "e4m3":
        vals = words.view(ml_dtypes.float8_e4m3fn).astype(np.float64)
    else:
        nib = np.empty((g, 128, n, 4), np.uint8)
        nib[..., 0::2] = words & 0xF
        nib[..., 1::2] = words >> 4
        vals = E2M1[nib]
    vals = vals * np.repeat(np.exp2(scales.astype(np.float64) - 127.0), 8, axis=1)[..., None]
    return vals.transpose(0, 1, 3, 2).reshape(g * 512, n)


def bf(x):
    return np.asarray(x, np.float32).astype(ml_dtypes.bfloat16)


def planes(Y):
    r, m = Y.shape
    b = f64(bf(Y)).reshape(r // 32, 32, m)
    amax = np.abs(b).max(1)
    byte = np.clip(np.where(amax > 0, np.frexp(amax)[1] - 1 + 127 - 7, 1), 1, 254)
    codes = (b * np.exp2(127.0 - byte)[:, None, :]).reshape(r, m).astype(np.float32).astype(ml_dtypes.float8_e4m3fn).view(np.uint8)
    words = codes.reshape(r // 512, 128, 4, m).transpose(0, 1, 3, 2)
    return np.ascontiguousarray(words), np.ascontiguousarray(byte.astype(np.uint8).reshape(r // 512, 16, m))


D, T, I, Q, E, M = 512, 1024, 512, 512, 512, 1024


def setup_inputs():
    n = np.random.standard_normal
    idx = np.random.permutation(T)[:I]
    idx2 = np.random.permutation(T)[:I]
    idx3 = np.random.permutation(T)[:I]
    idx4 = np.random.permutation(M)[:I]
    fd = mx_kscale(D)
    fq = mx_kscale(Q)
    keysp = pack_weight(n((D, T)) / fd[:, None], "e2m1")
    return {
        "query": (n((D, Q)) * 1.0 / np.sqrt(D) * fd[:, None]).astype(np.float32),
        "keys_words": keysp[0],
        "keys_scales": keysp[1],
        "lam": (np.random.uniform(0.4, 1.0, (Q, 1))).astype(np.float32),
        "qs": (np.random.uniform(0.5, 2.0, (Q, 1)) * fq[:, None]).astype(np.float32),
        "msgs": (n((Q, E)) * 1 / np.sqrt(Q) / fq[:, None]).astype(np.float32),
        "old": (n((E, M)) * 1.0).astype(np.float32),
        "offs": striped(idx),
        "offs2": striped(idx2),
        "offs3": striped(idx3),
        "offs4": striped(idx4),
    }


def reference(query, keys_words, keys_scales, lam, qs, msgs, old, offs, offs2, offs3, offs4):
    idx = unstriped(offs)
    idx2 = unstriped(offs2)
    idx3 = unstriped(offs3)
    idx4 = unstriped(offs4)
    keysu = unpack_weight(keys_words, keys_scales, "e2m1")
    queryq = mxq(f64(query), 0, "e4m3")
    a = queryq.T @ keysu
    w = a[:, idx] + np.tanh(a[:, idx2] - a[:, idx3]) * f64(lam)
    wq = w * f64(qs)
    msgsq = mxq(f64(msgs), 0, "e4m3")
    wqq = mxq(wq, 0, "e4m3")
    dl = msgsq.T @ wqq
    df = np.zeros((E, M))
    df[:, idx4] = dl
    y = f64(old) + df
    words, scales = planes(y)
    return y, words, scales

@@ -1,0 +1,285 @@
+from contextlib import ExitStack
+
+import concourse.mybir as mybir
+
+D, T, I, Q, E, M = 512, 1024, 512, 512, 512, 1024
+FLOPS = 2 * D * Q * T + 2 * Q * E * I
+
+F32 = mybir.dt.float32
+BF16 = mybir.dt.bfloat16
+I32 = mybir.dt.int32
+U32 = mybir.dt.uint32
+U16 = mybir.dt.uint16
+U8 = mybir.dt.uint8
+FP8X4 = mybir.dt.float8_e4m3fn_x4
+FP4X4 = mybir.dt.float4_e2m1fn_x4
+ALU = mybir.AluOpType
+ACT = mybir.ActivationFunctionType
+
+P = 128
+PACK = 4
+BANK = 512
+CHUNK = 256
+OUT_COLS = 256
+
+
+def tile_attend_seconded_deliveredplanes_lean_pl_kernel(
+    tc, query, keys_words, keys_scales, lam, qs, msgs, old, offs, offs2, offs3, offs4, out_0, out_1, out_2
+):
+    nc = tc.nc
+    chunks = I // CHUNK
+    with ExitStack() as ctx:
+        keep = ctx.enter_context(tc.tile_pool(name="keep", bufs=1))
+        psum = ctx.enter_context(tc.psum_pool(name="psum", bufs=8))
+
+        def sb(name, shape, dtype):
+            return keep.tile(shape, dtype, name=name, align_bytes=64)
+
+        own_list = keep.tile([P, I // 16], U16, name="own_list")
+        second_list = keep.tile([P, I // 16], U16, name="second_list")
+        oppose_list = keep.tile([P, I // 16], U16, name="oppose_list")
+        place_list = keep.tile([P, I // 16], U16, name="place_list")
+
+        def part(lst, c):
+            return lst[:, c * CHUNK // 16 : (c + 1) * CHUNK // 16]
+
+        key_scale = sb("key_scale", [P, T], U8)
+
+        lam_t = sb("lam_t", [P, PACK], F32)
+        qs_t = sb("qs_t", [P, PACK], F32)
+
+        half = Q // 2
+        query_rows = query.rearrange("(p j) q -> p j q", j=PACK)
+        q_raw = [sb("q_raw%d" % h, [P, PACK, half], F32) for h in range(2)]
+        for h in range(2):
+            nc.sync.dma_start(out=q_raw[h][:], in_=query_rows[:, :, h * half : (h + 1) * half])
+        key_words = sb("key_words", [P, 2 * T], U8)
+        nc.sync.dma_start(out=key_words[:].bitcast(I32), in_=keys_words[0].bitcast(I32))
+        for quad in range(4):
+            nc.scalar.dma_start(
+                out=key_scale[32 * quad : 32 * quad + 4, :].bitcast(I32),
+                in_=keys_scales[0, 4 * quad : 4 * quad + 4, :].bitcast(I32),
+            )
+        nc.scalar.dma_start(out=lam_t[:], in_=lam.rearrange("(p r) o -> p (r o)", r=PACK))
+        nc.scalar.dma_start(out=qs_t[:], in_=qs.rearrange("(p r) o -> p (r o)", r=PACK))
+        nc.sync.dma_start(oppose_list[:], offs3)
+        nc.sync.dma_start(own_list[:], offs)
+        nc.sync.dma_start(second_list[:], offs2)
+        m_raw = sb("m_raw", [P, PACK, E], F32)
+        nc.sync.dma_start(out=m_raw[:], in_=msgs.rearrange("(p j) e -> p j e", j=PACK))
+        nc.sync.dma_start(place_list[:], offs4)
+        old_rows = old.rearrange("(p r) m -> p r m", r=PACK)
+        old_t = [sb("old%d" % r, [P, M], F32) for r in range(PACK)]
+        for r in range(PACK):
+            nc.sync.dma_start(out=old_t[r][:], in_=old_rows[:, r, :])
+
+        placed = [sb("placed%d" % r, [P, M], F32) for r in range(PACK)]
+        for r in range(PACK):
+            nc.vector.memset(placed[r][:], 0.0)
+
+        def deal(copy, dealt, raw, s_out, s_in, n):
+            copy(
+                out=dealt[:, :, s_out : s_out + n, :].rearrange("p r s j -> p s j r"),
+                in_=raw[:].rearrange("p j (s r) -> p s j r", r=PACK)[:, s_in : s_in + n, :, :],
+            )
+
+        q_bf = sb("q_bf", [P, PACK, P, PACK], BF16)
+        deal(nc.vector.tensor_copy, q_bf, q_raw[0], 0, 0, 64)
+        deal(nc.vector.tensor_copy, q_bf, q_raw[1], 64, 0, 42)
+        deal(nc.scalar.copy, q_bf, q_raw[1], 106, 42, 22)
+        q_codes = sb("q_codes", [P, Q], U32)
+        q_scale = sb("q_scale", [P, Q], U8)
+        for r in range(PACK):
+            nc.vector.quantize_mx(
+                out=q_codes[:, r * P : (r + 1) * P].bitcast(FP8X4),
+                scales=q_scale[:, r * P : (r + 1) * P],
+                in_=q_bf[:, r, :, :].rearrange("p s j -> p (s j)"),
+            )
+
+        scores = [sb("scores%d" % r, [P, T], F32) for r in range(PACK)]
+
+        def score(r, copies):
+            for h in range(T // BANK):
+                acc = psum.tile([P, BANK], F32, name="acc")
+                nc.tensor.matmul_mx(
+                    out=acc[:],
+                    lhsT=q_codes[:, r * P : (r + 1) * P].bitcast(FP8X4),
+                    lhsT_scale=q_scale[:, r * P : (r + 1) * P],
+                    rhs=key_words[:, 2 * h * BANK : 2 * (h + 1) * BANK].bitcast(FP4X4),
+                    rhs_scale=key_scale[:, h * BANK : (h + 1) * BANK],
+                    start=True,
+                    stop=True,
+                )
+                copies[h](out=scores[r][:, h * BANK : (h + 1) * BANK], in_=acc[:])
+
+        opposed = [[sb("opposed%d_%d" % (c, r), [P, CHUNK], F32) for r in range(PACK)] for c in range(chunks)]
+        margin = [[sb("margin%d_%d" % (c, r), [P, CHUNK], F32) for r in range(PACK)] for c in range(chunks)]
+        support = [[sb("support%d_%d" % (c, r), [P, CHUNK], F32) for r in range(PACK)] for c in range(chunks)]
+        own = [[sb("own%d_%d" % (c, r), [P, CHUNK], F32) for r in range(PACK)] for c in range(chunks)]
+        weight = [[sb("weight%d_%d" % (c, r), [P, CHUNK], F32) for r in range(PACK)] for c in range(chunks)]
+        wq_rows = [sb("wq_rows%d" % c, [P, PACK, CHUNK], BF16) for c in range(chunks)]
+        wq_bf = [sb("wq_bf%d" % c, [P, CHUNK, PACK], BF16) for c in range(chunks)]
+        wq_codes = [sb("wq_codes%d" % c, [P, CHUNK], U32) for c in range(chunks)]
+        wq_scale = [sb("wq_scale%d" % c, [P, CHUNK], U8) for c in range(chunks)]
+        sums = [[sb("sums%d_%d" % (c, b), [P, 2, CHUNK], F32) for b in range(2)] for c in range(chunks)]
+
+        def gather_opposed(c, r):
+            nc.scalar.activation(out=opposed[c][r][:], in_=scores[r][:].indirect(part(oppose_list, c)), func=ACT.Copy)
+
+        def gather_own_vector(c, r):
+            nc.vector.tensor_copy(out=own[c][r][:], in_=scores[r][:].indirect(part(own_list, c)))
+
+        def gather_own_scalar(c, r):
+            nc.scalar.activation(out=own[c][r][:], in_=scores[r][:].indirect(part(own_list, c)), func=ACT.Copy)
+
+        def gather_margin(c, r):
+            nc.vector.tensor_tensor(
+                out=margin[c][r][:],
+                in0=scores[r][:].indirect(part(second_list, c)),
+                in1=opposed[c][r][:],
+                op=ALU.subtract,
+            )
+
+        def squash(c, r):
+            nc.scalar.activation(out=support[c][r][:], in_=margin[c][r][:], func=ACT.Tanh)
+
+        def weigh(c, r):
+            nc.vector.scalar_tensor_tensor(
+                out=weight[c][r][:],
+                in0=support[c][r][:],
+                scalar=lam_t[:, r : r + 1],
+                in1=own[c][r][:],
+                op0=ALU.mult,
+                op1=ALU.add,
+            )
+
+        def factor(c, r):
+            nc.vector.tensor_scalar(
+                out=wq_rows[c][:, r, :], in0=weight[c][r][:], scalar1=qs_t[:, r : r + 1], scalar2=None, op0=ALU.mult
+            )
+
+        def interleave(copy, dst, src):
+            copy(
+                out=dst.rearrange("p (c i) r -> p c r i", i=4),
+                in_=src.rearrange("p r (c i) -> p c r i", i=4),
+            )
+
+        def quantise_weights(c):
+            interleave(nc.vector.tensor_copy, wq_bf[c][:], wq_rows[c][:])
+            nc.vector.quantize_mx(
+                out=wq_codes[c][:].bitcast(FP8X4),
+                scales=wq_scale[c][:],
+                in_=wq_bf[c][:].rearrange("p x r -> p (x r)"),
+            )
+
+        m_bf = sb("m_bf", [P, PACK, P, PACK], BF16)
+        m_codes = sb("m_codes", [P, E], U32)
+        m_scale = sb("m_scale", [P, E], U8)
+
+        def carry(c, copies):
+            for b in range(2):
+                acc = psum.tile([P, 2, CHUNK], F32, name="acc")
+                for k in range(2):
+                    r = 2 * b + k
+                    nc.tensor.matmul_mx(
+                        out=acc[:, k, :],
+                        lhsT=m_codes[:, r * P : (r + 1) * P].bitcast(FP8X4),
+                        lhsT_scale=m_scale[:, r * P : (r + 1) * P],
+                        rhs=wq_codes[c][:].bitcast(FP8X4),
+                        rhs_scale=wq_scale[c][:],
+                        start=True,
+                        stop=True,
+                    )
+                copies[b](out=sums[c][b][:], in_=acc[:])
+
+        def place_vector(c, r):
+            nc.vector.tensor_copy(out=placed[r][:].indirect(part(place_list, c)), in_=sums[c][r // 2][:, r % 2, :])
+
+        def place_scalar(c, r):
+            nc.scalar.activation(
+                out=placed[r][:].indirect(part(place_list, c)), in_=sums[c][r // 2][:, r % 2, :], func=ACT.Copy
+            )
+
+        vcopy, scopy = nc.vector.tensor_copy, nc.scalar.copy
+
+        score(0, (vcopy, scopy))
+        gather_opposed(0, 0)
+        gather_own_vector(0, 0)
+        gather_margin(0, 0)
+        for r in range(1, PACK):
+            score(r, (scopy, scopy))
+            squash(0, r - 1)
+            gather_opposed(0, r)
+            weigh(0, r - 1)
+            gather_margin(0, r)
+            factor(0, r - 1)
+            gather_own_scalar(0, r)
+            if r == 2:
+                deal(vcopy, m_bf, m_raw, 0, 0, P)
+            if r == 3:
+                nc.vector.quantize_mx(
+                    out=m_codes[:].bitcast(FP8X4), scales=m_scale[:], in_=m_bf[:].rearrange("p r s j -> p (r s j)")
+                )
+        squash(0, PACK - 1)
+        weigh(0, PACK - 1)
+        factor(0, PACK - 1)
+        quantise_weights(0)
+
+        for r in range(PACK):
+            gather_opposed(1, r)
+            gather_own_vector(1, r)
+            gather_margin(1, r)
+        for r in range(PACK):
+            squash(1, r)
+            weigh(1, r)
+        carry(0, (scopy, scopy))
+        for r in range(PACK):
+            factor(1, r)
+        for r in range(1, PACK):
+            place_scalar(0, r)
+        quantise_weights(1)
+        place_vector(0, 0)
+        carry(1, (vcopy, scopy))
+
+        y = sb("y", [P, PACK, M], F32)
+        y_bf = [sb("y_bf%d" % k, [P, OUT_COLS, PACK], BF16) for k in range(M // OUT_COLS)]
+        y_codes = sb("y_codes", [P, M], U32)
+        y_scale = sb("y_scale", [P, M], U8)
+        out_rows = out_0.rearrange("(p r) m -> p r m", r=PACK)
+        out_words = out_1[0].rearrange("p c r -> p (c r)").bitcast(I32)
+
+        place_vector(1, 0)
+        for r in range(PACK - 1):
+            place_scalar(1, r + 1)
+            nc.vector.tensor_tensor(out=y[:, r, :], in0=old_t[r][:], in1=placed[r][:], op=ALU.add)
+            nc.sync.dma_start(out=out_rows[:, r, :], in_=y[:, r, :])
+        last = PACK - 1
+        for k in range(M // OUT_COLS):
+            cols = slice(k * OUT_COLS, (k + 1) * OUT_COLS)
+            nc.vector.tensor_tensor(out=y[:, last, cols], in0=old_t[last][:, cols], in1=placed[last][:, cols], op=ALU.add)
+        nc.sync.dma_start(out=out_rows[:, last, :], in_=y[:, last, :])
+
+        def round_out(copy, k):
+            interleave(copy, y_bf[k][:], y[:, :, k * OUT_COLS : (k + 1) * OUT_COLS])
+
+        def quantise_out(k):
+            cols = slice(k * OUT_COLS, (k + 1) * OUT_COLS)
+            nc.vector.quantize_mx(
+                out=y_codes[:, cols].bitcast(FP8X4), scales=y_scale[:, cols], in_=y_bf[k][:].rearrange("p x r -> p (x r)")
+            )
+            nc.sync.dma_start(out=out_words[:, cols], in_=y_codes[:, cols].bitcast(I32))
+
+        round_out(scopy, 0)
+        round_out(scopy, 1)
+        round_out(vcopy, 3)
+        quantise_out(0)
+        round_out(vcopy, 2)
+        quantise_out(3)
+        quantise_out(1)
+        quantise_out(2)
+        for quad in range(4):
+            queue = nc.scalar if quad % 2 else nc.sync
+            queue.dma_start(
+                out=out_2[0, 4 * quad : 4 * quad + 4, :].bitcast(I32),
+                in_=y_scale[32 * quad : 32 * quad + 4, :].bitcast(I32),
+            )

@@ -32,8 +32,8 @@ def tile_attend_seconded_deliveredplanes_lean_pl_kernel(
         keep = ctx.enter_context(tc.tile_pool(name="keep", bufs=1))
         psum = ctx.enter_context(tc.psum_pool(name="psum", bufs=8))
 
-        def sb(name, shape, dtype):
-            return keep.tile(shape, dtype, name=name, align_bytes=64)
+        def sb(name, shape, dtype, tag=""):
+            return keep.tile(shape, dtype, name=name, tag=tag or name, align_bytes=64)
 
         own_list = keep.tile([P, I // 16], U16, name="own_list")
         second_list = keep.tile([P, I // 16], U16, name="second_list")
@@ -47,6 +47,7 @@ def tile_attend_seconded_deliveredplanes_lean_pl_kernel(
 
         lam_t = sb("lam_t", [P, PACK], F32)
         qs_t = sb("qs_t", [P, PACK], F32)
+        nc.scalar.dma_start(out=qs_t[:], in_=qs.rearrange("(p r) o -> p (r o)", r=PACK))
 
         half = Q // 2
         query_rows = query.rearrange("(p j) q -> p j q", j=PACK)
@@ -56,15 +57,14 @@ def tile_attend_seconded_deliveredplanes_lean_pl_kernel(
         key_words = sb("key_words", [P, 2 * T], U8)
         nc.sync.dma_start(out=key_words[:].bitcast(I32), in_=keys_words[0].bitcast(I32))
         for quad in range(4):
-            nc.scalar.dma_start(
+            (nc.scalar if quad < 3 else nc.sync).dma_start(
                 out=key_scale[32 * quad : 32 * quad + 4, :].bitcast(I32),
                 in_=keys_scales[0, 4 * quad : 4 * quad + 4, :].bitcast(I32),
             )
-        nc.scalar.dma_start(out=lam_t[:], in_=lam.rearrange("(p r) o -> p (r o)", r=PACK))
-        nc.scalar.dma_start(out=qs_t[:], in_=qs.rearrange("(p r) o -> p (r o)", r=PACK))
         nc.sync.dma_start(oppose_list[:], offs3)
-        nc.sync.dma_start(own_list[:], offs)
         nc.sync.dma_start(second_list[:], offs2)
+        nc.sync.dma_start(own_list[:], offs)
+        nc.sync.dma_start(out=lam_t[:], in_=lam.rearrange("(p r) o -> p (r o)", r=PACK))
         m_raw = sb("m_raw", [P, PACK, E], F32)
         nc.sync.dma_start(out=m_raw[:], in_=msgs.rearrange("(p j) e -> p j e", j=PACK))
         nc.sync.dma_start(place_list[:], offs4)
@@ -75,7 +75,7 @@ def tile_attend_seconded_deliveredplanes_lean_pl_kernel(
 
         placed = [sb("placed%d" % r, [P, M], F32) for r in range(PACK)]
         for r in range(PACK):
-            nc.vector.memset(placed[r][:], 0.0)
+            (nc.vector if r < 2 else nc.gpsimd).memset(placed[r][:], 0.0)
 
         def deal(copy, dealt, raw, s_out, s_in, n):
             copy(
@@ -96,66 +96,64 @@ def tile_attend_seconded_deliveredplanes_lean_pl_kernel(
                 in_=q_bf[:, r, :, :].rearrange("p s j -> p (s j)"),
             )
 
+        qs_wide = sb("qs_wide", [P, PACK, CHUNK], F32)
+        nc.scalar.copy(out=qs_wide[:], in_=qs_t[:].unsqueeze(2).to_broadcast([P, PACK, CHUNK]))
+        lam_qs = sb("lam_qs", [P, PACK], F32)
+        nc.vector.tensor_tensor(out=lam_qs[:], in0=lam_t[:], in1=qs_t[:], op=ALU.mult)
+
         scores = [sb("scores%d" % r, [P, T], F32) for r in range(PACK)]
 
         def score(r, copies):
-            for h in range(T // BANK):
-                acc = psum.tile([P, BANK], F32, name="acc")
+            n = T // len(copies)
+            for h, copy in enumerate(copies):
+                acc = psum.tile([P, n], F32, name="acc")
                 nc.tensor.matmul_mx(
                     out=acc[:],
                     lhsT=q_codes[:, r * P : (r + 1) * P].bitcast(FP8X4),
                     lhsT_scale=q_scale[:, r * P : (r + 1) * P],
-                    rhs=key_words[:, 2 * h * BANK : 2 * (h + 1) * BANK].bitcast(FP4X4),
-                    rhs_scale=key_scale[:, h * BANK : (h + 1) * BANK],
+                    rhs=key_words[:, 2 * h * n : 2 * (h + 1) * n].bitcast(FP4X4),
+                    rhs_scale=key_scale[:, h * n : (h + 1) * n],
                     start=True,
                     stop=True,
                 )
-                copies[h](out=scores[r][:, h * BANK : (h + 1) * BANK], in_=acc[:])
+                copy(out=scores[r][:, h * n : (h + 1) * n], in_=acc[:])
 
-        opposed = [[sb("opposed%d_%d" % (c, r), [P, CHUNK], F32) for r in range(PACK)] for c in range(chunks)]
-        margin = [[sb("margin%d_%d" % (c, r), [P, CHUNK], F32) for r in range(PACK)] for c in range(chunks)]
+        opposed = [sb("opposed", [P, PACK, CHUNK], F32)]
+        margin = [sb("margin0", [P, PACK, CHUNK], F32)]
         support = [[sb("support%d_%d" % (c, r), [P, CHUNK], F32) for r in range(PACK)] for c in range(chunks)]
-        own = [[sb("own%d_%d" % (c, r), [P, CHUNK], F32) for r in range(PACK)] for c in range(chunks)]
-        weight = [[sb("weight%d_%d" % (c, r), [P, CHUNK], F32) for r in range(PACK)] for c in range(chunks)]
+        own = [sb("own0", [P, PACK, CHUNK], F32)]
         wq_rows = [sb("wq_rows%d" % c, [P, PACK, CHUNK], BF16) for c in range(chunks)]
         wq_bf = [sb("wq_bf%d" % c, [P, CHUNK, PACK], BF16) for c in range(chunks)]
         wq_codes = [sb("wq_codes%d" % c, [P, CHUNK], U32) for c in range(chunks)]
         wq_scale = [sb("wq_scale%d" % c, [P, CHUNK], U8) for c in range(chunks)]
-        sums = [[sb("sums%d_%d" % (c, b), [P, 2, CHUNK], F32) for b in range(2)] for c in range(chunks)]
 
         def gather_opposed(c, r):
-            nc.scalar.activation(out=opposed[c][r][:], in_=scores[r][:].indirect(part(oppose_list, c)), func=ACT.Copy)
+            nc.scalar.activation(out=opposed[c][:, r, :], in_=scores[r][:].indirect(part(oppose_list, c)), func=ACT.Copy)
 
-        def gather_own_vector(c, r):
-            nc.vector.tensor_copy(out=own[c][r][:], in_=scores[r][:].indirect(part(own_list, c)))
-
-        def gather_own_scalar(c, r):
-            nc.scalar.activation(out=own[c][r][:], in_=scores[r][:].indirect(part(own_list, c)), func=ACT.Copy)
+        def gather_own(c, r):
+            nc.vector.tensor_tensor(
+                out=own[c][:, r, :], in0=scores[r][:].indirect(part(own_list, c)), in1=qs_wide[:, r, :], op=ALU.mult
+            )
 
         def gather_margin(c, r):
             nc.vector.tensor_tensor(
-                out=margin[c][r][:],
+                out=margin[c][:, r, :],
                 in0=scores[r][:].indirect(part(second_list, c)),
-                in1=opposed[c][r][:],
+                in1=opposed[c][:, r, :],
                 op=ALU.subtract,
             )
 
         def squash(c, r):
-            nc.scalar.activation(out=support[c][r][:], in_=margin[c][r][:], func=ACT.Tanh)
+            nc.scalar.activation(out=support[c][r][:], in_=margin[c][:, r, :], func=ACT.Tanh)
 
         def weigh(c, r):
             nc.vector.scalar_tensor_tensor(
-                out=weight[c][r][:],
+                out=wq_rows[c][:, r, :],
                 in0=support[c][r][:],
-                scalar=lam_t[:, r : r + 1],
-                in1=own[c][r][:],
+                scalar=lam_qs[:, r : r + 1],
+                in1=own[c][:, r, :],
                 op0=ALU.mult,
                 op1=ALU.add,
-            )
-
-        def factor(c, r):
-            nc.vector.tensor_scalar(
-                out=wq_rows[c][:, r, :], in0=weight[c][r][:], scalar1=qs_t[:, r : r + 1], scalar2=None, op0=ALU.mult
             )
 
         def interleave(copy, dst, src):
@@ -176,45 +174,48 @@ def tile_attend_seconded_deliveredplanes_lean_pl_kernel(
         m_codes = sb("m_codes", [P, E], U32)
         m_scale = sb("m_scale", [P, E], U8)
 
-        def carry(c, copies):
-            for b in range(2):
-                acc = psum.tile([P, 2, CHUNK], F32, name="acc")
-                for k in range(2):
-                    r = 2 * b + k
-                    nc.tensor.matmul_mx(
-                        out=acc[:, k, :],
-                        lhsT=m_codes[:, r * P : (r + 1) * P].bitcast(FP8X4),
-                        lhsT_scale=m_scale[:, r * P : (r + 1) * P],
-                        rhs=wq_codes[c][:].bitcast(FP8X4),
-                        rhs_scale=wq_scale[c][:],
-                        start=True,
-                        stop=True,
-                    )
-                copies[b](out=sums[c][b][:], in_=acc[:])
+        def carry(c, tiles):
+            acc = psum.tile([P, len(tiles), CHUNK], F32, name="acc")
+            for k, r in enumerate(tiles):
+                nc.tensor.matmul_mx(
+                    out=acc[:, k, :],
+                    lhsT=m_codes[:, r * P : (r + 1) * P].bitcast(FP8X4),
+                    lhsT_scale=m_scale[:, r * P : (r + 1) * P],
+                    rhs=wq_codes[c][:].bitcast(FP8X4),
+                    rhs_scale=wq_scale[c][:],
+                    start=True,
+                    stop=True,
+                )
+            return acc
+
+        sums = {}
+
+        def drain(copy, acc, c, tiles, tag=""):
+            staged = sb("sums%d_%d" % (c, tiles[0]), [P, len(tiles), CHUNK], F32, tag=tag)
+            copy(out=staged[:], in_=acc[:])
+            for k, r in enumerate(tiles):
+                sums[c, r] = staged[:, k, :]
 
         def place_vector(c, r):
-            nc.vector.tensor_copy(out=placed[r][:].indirect(part(place_list, c)), in_=sums[c][r // 2][:, r % 2, :])
+            nc.vector.tensor_copy(out=placed[r][:].indirect(part(place_list, c)), in_=sums[c, r])
 
         def place_scalar(c, r):
-            nc.scalar.activation(
-                out=placed[r][:].indirect(part(place_list, c)), in_=sums[c][r // 2][:, r % 2, :], func=ACT.Copy
-            )
+            nc.scalar.activation(out=placed[r][:].indirect(part(place_list, c)), in_=sums[c, r], func=ACT.Copy)
 
         vcopy, scopy = nc.vector.tensor_copy, nc.scalar.copy
 
-        score(0, (vcopy, scopy))
+        score(0, (vcopy, scopy, vcopy, scopy))
         gather_opposed(0, 0)
-        gather_own_vector(0, 0)
+        gather_own(0, 0)
         gather_margin(0, 0)
         for r in range(1, PACK):
             score(r, (scopy, scopy))
-            squash(0, r - 1)
             gather_opposed(0, r)
-            weigh(0, r - 1)
+            squash(0, r - 1)
             gather_margin(0, r)
-            factor(0, r - 1)
-            gather_own_scalar(0, r)
-            if r == 2:
+            gather_own(0, r)
+            weigh(0, r - 1)
+            if r == 1:
                 deal(vcopy, m_bf, m_raw, 0, 0, P)
             if r == 3:
                 nc.vector.quantize_mx(
@@ -222,24 +223,31 @@ def tile_attend_seconded_deliveredplanes_lean_pl_kernel(
                 )
         squash(0, PACK - 1)
         weigh(0, PACK - 1)
-        factor(0, PACK - 1)
         quantise_weights(0)
 
+        opposed.append(sb("opposed1", [P, PACK, CHUNK], F32, tag="opposed"))
+        margin.append(sb("margin1", [P, PACK, CHUNK], F32, tag="wq_rows0"))
+        own.append(sb("own1", [P, PACK, CHUNK], F32, tag="wq_bf0"))
         for r in range(PACK):
             gather_opposed(1, r)
-            gather_own_vector(1, r)
             gather_margin(1, r)
+        drain(scopy, carry(0, (1, 2)), 0, (1, 2))
+        drain(scopy, carry(0, (3,)), 0, (3,))
+        held = carry(0, (0,))
         for r in range(PACK):
             squash(1, r)
-            weigh(1, r)
-        carry(0, (scopy, scopy))
         for r in range(PACK):
-            factor(1, r)
+            gather_own(1, r)
+            weigh(1, r)
         for r in range(1, PACK):
             place_scalar(0, r)
         quantise_weights(1)
+        drain(vcopy, held, 0, (0,), tag="wq_bf1")
         place_vector(0, 0)
-        carry(1, (vcopy, scopy))
+        drain(scopy, carry(1, (1, 0)), 1, (1, 0))
+        place_vector(1, 0)
+        place_scalar(1, 1)
+        drain(scopy, carry(1, (2, 3)), 1, (2, 3))
 
         y = sb("y", [P, PACK, M], F32)
         y_bf = [sb("y_bf%d" % k, [P, OUT_COLS, PACK], BF16) for k in range(M // OUT_COLS)]
@@ -248,9 +256,9 @@ def tile_attend_seconded_deliveredplanes_lean_pl_kernel(
         out_rows = out_0.rearrange("(p r) m -> p r m", r=PACK)
         out_words = out_1[0].rearrange("p c r -> p (c r)").bitcast(I32)
 
-        place_vector(1, 0)
         for r in range(PACK - 1):
-            place_scalar(1, r + 1)
+            if r:
+                place_scalar(1, r + 1)
             nc.vector.tensor_tensor(out=y[:, r, :], in0=old_t[r][:], in1=placed[r][:], op=ALU.add)
             nc.sync.dma_start(out=out_rows[:, r, :], in_=y[:, r, :])
         last = PACK - 1
@@ -271,12 +279,10 @@ def tile_attend_seconded_deliveredplanes_lean_pl_kernel(
 
         round_out(scopy, 0)
         round_out(scopy, 1)
-        round_out(vcopy, 3)
-        quantise_out(0)
         round_out(vcopy, 2)
-        quantise_out(3)
-        quantise_out(1)
-        quantise_out(2)
+        round_out(vcopy, 3)
+        for k in (0, 2, 3, 1):
+            quantise_out(k)
         for quad in range(4):
             queue = nc.scalar if quad % 2 else nc.sync
             queue.dma_start(

@@ -21,6 +21,7 @@ PACK = 4
 BANK = 512
 CHUNK = 256
 OUT_COLS = 256
+POOL_COLS = 512
 
 
 def tile_attend_seconded_deliveredplanes_lean_pl_kernel(
@@ -118,8 +119,8 @@ def tile_attend_seconded_deliveredplanes_lean_pl_kernel(
                 )
                 copy(out=scores[r][:, h * n : (h + 1) * n], in_=acc[:])
 
-        opposed = [sb("opposed", [P, PACK, CHUNK], F32)]
-        margin = [sb("margin0", [P, PACK, CHUNK], F32)]
+        opposed = [[sb("opposed0_%d" % r, [P, CHUNK], F32)[:] for r in range(PACK)]]
+        margin = [[sb("margin0_%d" % r, [P, CHUNK], F32)[:] for r in range(PACK)]]
         support = [[sb("support%d_%d" % (c, r), [P, CHUNK], F32) for r in range(PACK)] for c in range(chunks)]
         own = [sb("own0", [P, PACK, CHUNK], F32)]
         wq_rows = [sb("wq_rows%d" % c, [P, PACK, CHUNK], BF16) for c in range(chunks)]
@@ -128,7 +129,7 @@ def tile_attend_seconded_deliveredplanes_lean_pl_kernel(
         wq_scale = [sb("wq_scale%d" % c, [P, CHUNK], U8) for c in range(chunks)]
 
         def gather_opposed(c, r):
-            nc.scalar.activation(out=opposed[c][:, r, :], in_=scores[r][:].indirect(part(oppose_list, c)), func=ACT.Copy)
+            nc.scalar.activation(out=opposed[c][r], in_=scores[r][:].indirect(part(oppose_list, c)), func=ACT.Copy)
 
         def gather_own(c, r):
             nc.vector.tensor_tensor(
@@ -137,14 +138,14 @@ def tile_attend_seconded_deliveredplanes_lean_pl_kernel(
 
         def gather_margin(c, r):
             nc.vector.tensor_tensor(
-                out=margin[c][:, r, :],
+                out=margin[c][r],
                 in0=scores[r][:].indirect(part(second_list, c)),
-                in1=opposed[c][:, r, :],
+                in1=opposed[c][r],
                 op=ALU.subtract,
             )
 
         def squash(c, r):
-            nc.scalar.activation(out=support[c][r][:], in_=margin[c][:, r, :], func=ACT.Tanh)
+            nc.scalar.activation(out=support[c][r][:], in_=margin[c][r], func=ACT.Tanh)
 
         def weigh(c, r):
             nc.vector.scalar_tensor_tensor(
@@ -163,12 +164,15 @@ def tile_attend_seconded_deliveredplanes_lean_pl_kernel(
             )
 
         def quantise_weights(c):
-            interleave(nc.vector.tensor_copy, wq_bf[c][:], wq_rows[c][:])
-            nc.vector.quantize_mx(
-                out=wq_codes[c][:].bitcast(FP8X4),
-                scales=wq_scale[c][:],
-                in_=wq_bf[c][:].rearrange("p x r -> p (x r)"),
-            )
+            halves = [slice(h * P, (h + 1) * P) for h in range(CHUNK // P)]
+            for cols in halves:
+                interleave(nc.vector.tensor_copy, wq_bf[c][:, cols, :], wq_rows[c][:, :, cols])
+            for cols in halves:
+                nc.vector.quantize_mx(
+                    out=wq_codes[c][:, cols].bitcast(FP8X4),
+                    scales=wq_scale[c][:, cols],
+                    in_=wq_bf[c][:, cols, :].rearrange("p x r -> p (x r)"),
+                )
 
         m_bf = sb("m_bf", [P, PACK, P, PACK], BF16)
         m_codes = sb("m_codes", [P, E], U32)
@@ -225,29 +229,35 @@ def tile_attend_seconded_deliveredplanes_lean_pl_kernel(
         weigh(0, PACK - 1)
         quantise_weights(0)
 
-        opposed.append(sb("opposed1", [P, PACK, CHUNK], F32, tag="opposed"))
-        margin.append(sb("margin1", [P, PACK, CHUNK], F32, tag="wq_rows0"))
+        def first_and_rest(name, first_tag, rest_tag):
+            first = sb(name + "_first", [P, CHUNK], F32, tag=first_tag)
+            rest = sb(name + "_rest", [P, PACK - 1, CHUNK], F32, tag=rest_tag)
+            return [first[:]] + [rest[:, k, :] for k in range(PACK - 1)]
+
+        opposed.append(first_and_rest("opposed1", "margin0_2", "margin0_3"))
+        margin.append(first_and_rest("margin1", "", "wq_rows0"))
         own.append(sb("own1", [P, PACK, CHUNK], F32, tag="wq_bf0"))
         for r in range(PACK):
             gather_opposed(1, r)
             gather_margin(1, r)
-        drain(scopy, carry(0, (1, 2)), 0, (1, 2))
-        drain(scopy, carry(0, (3,)), 0, (3,))
-        held = carry(0, (0,))
+        drain(scopy, carry(0, (0, 1)), 0, (0, 1))
+        drain(scopy, carry(0, (2,)), 0, (2,))
+        held = carry(0, (3,))
         for r in range(PACK):
             squash(1, r)
         for r in range(PACK):
             gather_own(1, r)
             weigh(1, r)
-        for r in range(1, PACK):
+        for r in range(PACK - 1):
             place_scalar(0, r)
         quantise_weights(1)
-        drain(vcopy, held, 0, (0,), tag="wq_bf1")
-        place_vector(0, 0)
-        drain(scopy, carry(1, (1, 0)), 1, (1, 0))
+        drain(vcopy, held, 0, (3,), tag="wq_bf1")
+        drain(scopy, carry(1, (1,)), 1, (1,))
+        drain(vcopy, carry(1, (0,)), 1, (0,))
+        place_vector(0, 3)
         place_vector(1, 0)
         place_scalar(1, 1)
-        drain(scopy, carry(1, (2, 3)), 1, (2, 3))
+        drain(scopy, carry(1, (2, 3)), 1, (2, 3), tag="sums1_1")
 
         y = sb("y", [P, PACK, M], F32)
         y_bf = [sb("y_bf%d" % k, [P, OUT_COLS, PACK], BF16) for k in range(M // OUT_COLS)]
@@ -256,15 +266,21 @@ def tile_attend_seconded_deliveredplanes_lean_pl_kernel(
         out_rows = out_0.rearrange("(p r) m -> p r m", r=PACK)
         out_words = out_1[0].rearrange("p c r -> p (c r)").bitcast(I32)
 
-        for r in range(PACK - 1):
-            if r:
-                place_scalar(1, r + 1)
-            nc.vector.tensor_tensor(out=y[:, r, :], in0=old_t[r][:], in1=placed[r][:], op=ALU.add)
+        def add_old(engine, r, cols):
+            engine.tensor_tensor(out=y[:, r, cols], in0=old_t[r][:, cols], in1=placed[r][:, cols], op=ALU.add)
+
+        place_scalar(1, 2)
+        place_scalar(1, 3)
+        add_old(nc.gpsimd, 1, slice(0, POOL_COLS))
+        add_old(nc.vector, 1, slice(POOL_COLS, M))
+        nc.sync.dma_start(out=out_rows[:, 1, :], in_=y[:, 1, :])
+        for r in (0, 2):
+            add_old(nc.vector, r, slice(0, M))
             nc.sync.dma_start(out=out_rows[:, r, :], in_=y[:, r, :])
         last = PACK - 1
         for k in range(M // OUT_COLS):
             cols = slice(k * OUT_COLS, (k + 1) * OUT_COLS)
-            nc.vector.tensor_tensor(out=y[:, last, cols], in0=old_t[last][:, cols], in1=placed[last][:, cols], op=ALU.add)
+            add_old(nc.vector, last, cols)
         nc.sync.dma_start(out=out_rows[:, last, :], in_=y[:, last, :])
 
         def round_out(copy, k):
@@ -275,14 +291,16 @@ def tile_attend_seconded_deliveredplanes_lean_pl_kernel(
             nc.vector.quantize_mx(
                 out=y_codes[:, cols].bitcast(FP8X4), scales=y_scale[:, cols], in_=y_bf[k][:].rearrange("p x r -> p (x r)")
             )
-            nc.sync.dma_start(out=out_words[:, cols], in_=y_codes[:, cols].bitcast(I32))
 
         round_out(scopy, 0)
-        round_out(scopy, 1)
+        round_out(scopy, 3)
+        round_out(vcopy, 1)
         round_out(vcopy, 2)
-        round_out(vcopy, 3)
-        for k in (0, 2, 3, 1):
-            quantise_out(k)
+        for pieces in ((0, 1), (2,), (3,)):
+            for k in pieces:
+                quantise_out(k)
+            cols = slice(pieces[0] * OUT_COLS, (pieces[-1] + 1) * OUT_COLS)
+            nc.sync.dma_start(out=out_words[:, cols], in_=y_codes[:, cols].bitcast(I32))
         for quad in range(4):
             queue = nc.scalar if quad % 2 else nc.sync
             queue.dma_start(

from contextlib import ExitStack

import concourse.mybir as mybir

D, T, I, Q, E, M = 512, 1024, 512, 512, 512, 1024
FLOPS = 2 * D * Q * T + 2 * Q * E * I

F32 = mybir.dt.float32
BF16 = mybir.dt.bfloat16
I32 = mybir.dt.int32
U32 = mybir.dt.uint32
U16 = mybir.dt.uint16
U8 = mybir.dt.uint8
FP8X4 = mybir.dt.float8_e4m3fn_x4
FP4X4 = mybir.dt.float4_e2m1fn_x4
ALU = mybir.AluOpType
ACT = mybir.ActivationFunctionType

P = 128
PACK = 4
BANK = 512
CHUNK = 256
OUT_COLS = 256
POOL_COLS = 512


def tile_attend_seconded_deliveredplanes_lean_pl_kernel(
    tc, query, keys_words, keys_scales, lam, qs, msgs, old, offs, offs2, offs3, offs4, out_0, out_1, out_2
):
    nc = tc.nc
    chunks = I // CHUNK
    with ExitStack() as ctx:
        keep = ctx.enter_context(tc.tile_pool(name="keep", bufs=1))
        psum = ctx.enter_context(tc.psum_pool(name="psum", bufs=8))

        def sb(name, shape, dtype, tag=""):
            return keep.tile(shape, dtype, name=name, tag=tag or name, align_bytes=64)

        own_list = keep.tile([P, I // 16], U16, name="own_list")
        second_list = keep.tile([P, I // 16], U16, name="second_list")
        oppose_list = keep.tile([P, I // 16], U16, name="oppose_list")
        place_list = keep.tile([P, I // 16], U16, name="place_list")

        def part(lst, c):
            return lst[:, c * CHUNK // 16 : (c + 1) * CHUNK // 16]

        key_scale = sb("key_scale", [P, T], U8)

        lam_t = sb("lam_t", [P, PACK], F32)
        qs_t = sb("qs_t", [P, PACK], F32)
        nc.scalar.dma_start(out=qs_t[:], in_=qs.rearrange("(p r) o -> p (r o)", r=PACK))

        half = Q // 2
        query_rows = query.rearrange("(p j) q -> p j q", j=PACK)
        q_raw = [sb("q_raw%d" % h, [P, PACK, half], F32) for h in range(2)]
        for h in range(2):
            nc.sync.dma_start(out=q_raw[h][:], in_=query_rows[:, :, h * half : (h + 1) * half])
        key_words = sb("key_words", [P, 2 * T], U8)
        nc.sync.dma_start(out=key_words[:].bitcast(I32), in_=keys_words[0].bitcast(I32))
        for quad in range(4):
            (nc.scalar if quad < 3 else nc.sync).dma_start(
                out=key_scale[32 * quad : 32 * quad + 4, :].bitcast(I32),
                in_=keys_scales[0, 4 * quad : 4 * quad + 4, :].bitcast(I32),
            )
        nc.sync.dma_start(oppose_list[:], offs3)
        nc.sync.dma_start(second_list[:], offs2)
        nc.sync.dma_start(own_list[:], offs)
        nc.sync.dma_start(out=lam_t[:], in_=lam.rearrange("(p r) o -> p (r o)", r=PACK))
        m_raw = sb("m_raw", [P, PACK, E], F32)
        nc.sync.dma_start(out=m_raw[:], in_=msgs.rearrange("(p j) e -> p j e", j=PACK))
        nc.sync.dma_start(place_list[:], offs4)
        old_rows = old.rearrange("(p r) m -> p r m", r=PACK)
        old_t = [sb("old%d" % r, [P, M], F32) for r in range(PACK)]
        for r in range(PACK):
            nc.sync.dma_start(out=old_t[r][:], in_=old_rows[:, r, :])

        placed = [sb("placed%d" % r, [P, M], F32) for r in range(PACK)]
        for r in range(PACK):
            (nc.vector if r < 2 else nc.gpsimd).memset(placed[r][:], 0.0)

        def deal(copy, dealt, raw, s_out, s_in, n):
            copy(
                out=dealt[:, :, s_out : s_out + n, :].rearrange("p r s j -> p s j r"),
                in_=raw[:].rearrange("p j (s r) -> p s j r", r=PACK)[:, s_in : s_in + n, :, :],
            )

        q_bf = sb("q_bf", [P, PACK, P, PACK], BF16)
        deal(nc.vector.tensor_copy, q_bf, q_raw[0], 0, 0, 64)
        deal(nc.vector.tensor_copy, q_bf, q_raw[1], 64, 0, 42)
        deal(nc.scalar.copy, q_bf, q_raw[1], 106, 42, 22)
        q_codes = sb("q_codes", [P, Q], U32)
        q_scale = sb("q_scale", [P, Q], U8)
        for r in range(PACK):
            nc.vector.quantize_mx(
                out=q_codes[:, r * P : (r + 1) * P].bitcast(FP8X4),
                scales=q_scale[:, r * P : (r + 1) * P],
                in_=q_bf[:, r, :, :].rearrange("p s j -> p (s j)"),
            )

        qs_wide = sb("qs_wide", [P, PACK, CHUNK], F32)
        nc.scalar.copy(out=qs_wide[:], in_=qs_t[:].unsqueeze(2).to_broadcast([P, PACK, CHUNK]))
        lam_qs = sb("lam_qs", [P, PACK], F32)
        nc.vector.tensor_tensor(out=lam_qs[:], in0=lam_t[:], in1=qs_t[:], op=ALU.mult)

        scores = [sb("scores%d" % r, [P, T], F32) for r in range(PACK)]

        def score(r, copies):
            n = T // len(copies)
            for h, copy in enumerate(copies):
                acc = psum.tile([P, n], F32, name="acc")
                nc.tensor.matmul_mx(
                    out=acc[:],
                    lhsT=q_codes[:, r * P : (r + 1) * P].bitcast(FP8X4),
                    lhsT_scale=q_scale[:, r * P : (r + 1) * P],
                    rhs=key_words[:, 2 * h * n : 2 * (h + 1) * n].bitcast(FP4X4),
                    rhs_scale=key_scale[:, h * n : (h + 1) * n],
                    start=True,
                    stop=True,
                )
                copy(out=scores[r][:, h * n : (h + 1) * n], in_=acc[:])

        opposed = [[sb("opposed0_%d" % r, [P, CHUNK], F32)[:] for r in range(PACK)]]
        margin = [[sb("margin0_%d" % r, [P, CHUNK], F32)[:] for r in range(PACK)]]
        support = [[sb("support%d_%d" % (c, r), [P, CHUNK], F32) for r in range(PACK)] for c in range(chunks)]
        own = [sb("own0", [P, PACK, CHUNK], F32)]
        wq_rows = [sb("wq_rows%d" % c, [P, PACK, CHUNK], BF16) for c in range(chunks)]
        wq_bf = [sb("wq_bf%d" % c, [P, CHUNK, PACK], BF16) for c in range(chunks)]
        wq_codes = [sb("wq_codes%d" % c, [P, CHUNK], U32) for c in range(chunks)]
        wq_scale = [sb("wq_scale%d" % c, [P, CHUNK], U8) for c in range(chunks)]

        def gather_opposed(c, r):
            nc.scalar.activation(out=opposed[c][r], in_=scores[r][:].indirect(part(oppose_list, c)), func=ACT.Copy)

        def gather_own(c, r):
            nc.vector.tensor_tensor(
                out=own[c][:, r, :], in0=scores[r][:].indirect(part(own_list, c)), in1=qs_wide[:, r, :], op=ALU.mult
            )

        def gather_margin(c, r):
            nc.vector.tensor_tensor(
                out=margin[c][r],
                in0=scores[r][:].indirect(part(second_list, c)),
                in1=opposed[c][r],
                op=ALU.subtract,
            )

        def squash(c, r):
            nc.scalar.activation(out=support[c][r][:], in_=margin[c][r], func=ACT.Tanh)

        def weigh(c, r):
            nc.vector.scalar_tensor_tensor(
                out=wq_rows[c][:, r, :],
                in0=support[c][r][:],
                scalar=lam_qs[:, r : r + 1],
                in1=own[c][:, r, :],
                op0=ALU.mult,
                op1=ALU.add,
            )

        def interleave(copy, dst, src):
            copy(
                out=dst.rearrange("p (c i) r -> p c r i", i=4),
                in_=src.rearrange("p r (c i) -> p c r i", i=4),
            )

        def quantise_weights(c):
            halves = [slice(h * P, (h + 1) * P) for h in range(CHUNK // P)]
            for cols in halves:
                interleave(nc.vector.tensor_copy, wq_bf[c][:, cols, :], wq_rows[c][:, :, cols])
            for cols in halves:
                nc.vector.quantize_mx(
                    out=wq_codes[c][:, cols].bitcast(FP8X4),
                    scales=wq_scale[c][:, cols],
                    in_=wq_bf[c][:, cols, :].rearrange("p x r -> p (x r)"),
                )

        m_bf = sb("m_bf", [P, PACK, P, PACK], BF16)
        m_codes = sb("m_codes", [P, E], U32)
        m_scale = sb("m_scale", [P, E], U8)

        def carry(c, tiles):
            acc = psum.tile([P, len(tiles), CHUNK], F32, name="acc")
            for k, r in enumerate(tiles):
                nc.tensor.matmul_mx(
                    out=acc[:, k, :],
                    lhsT=m_codes[:, r * P : (r + 1) * P].bitcast(FP8X4),
                    lhsT_scale=m_scale[:, r * P : (r + 1) * P],
                    rhs=wq_codes[c][:].bitcast(FP8X4),
                    rhs_scale=wq_scale[c][:],
                    start=True,
                    stop=True,
                )
            return acc

        sums = {}

        def drain(copy, acc, c, tiles, tag=""):
            staged = sb("sums%d_%d" % (c, tiles[0]), [P, len(tiles), CHUNK], F32, tag=tag)
            copy(out=staged[:], in_=acc[:])
            for k, r in enumerate(tiles):
                sums[c, r] = staged[:, k, :]

        def place_vector(c, r):
            nc.vector.tensor_copy(out=placed[r][:].indirect(part(place_list, c)), in_=sums[c, r])

        def place_scalar(c, r):
            nc.scalar.activation(out=placed[r][:].indirect(part(place_list, c)), in_=sums[c, r], func=ACT.Copy)

        vcopy, scopy = nc.vector.tensor_copy, nc.scalar.copy

        score(0, (vcopy, scopy, vcopy, scopy))
        gather_opposed(0, 0)
        gather_own(0, 0)
        gather_margin(0, 0)
        for r in range(1, PACK):
            score(r, (scopy, scopy))
            gather_opposed(0, r)
            squash(0, r - 1)
            gather_margin(0, r)
            gather_own(0, r)
            weigh(0, r - 1)
            if r == 1:
                deal(vcopy, m_bf, m_raw, 0, 0, P)
            if r == 3:
                nc.vector.quantize_mx(
                    out=m_codes[:].bitcast(FP8X4), scales=m_scale[:], in_=m_bf[:].rearrange("p r s j -> p (r s j)")
                )
        squash(0, PACK - 1)
        weigh(0, PACK - 1)
        quantise_weights(0)

        def first_and_rest(name, first_tag, rest_tag):
            first = sb(name + "_first", [P, CHUNK], F32, tag=first_tag)
            rest = sb(name + "_rest", [P, PACK - 1, CHUNK], F32, tag=rest_tag)
            return [first[:]] + [rest[:, k, :] for k in range(PACK - 1)]

        opposed.append(first_and_rest("opposed1", "margin0_2", "margin0_3"))
        margin.append(first_and_rest("margin1", "", "wq_rows0"))
        own.append(sb("own1", [P, PACK, CHUNK], F32, tag="wq_bf0"))
        for r in range(PACK):
            gather_opposed(1, r)
            gather_margin(1, r)
        drain(scopy, carry(0, (0, 1)), 0, (0, 1))
        drain(scopy, carry(0, (2,)), 0, (2,))
        held = carry(0, (3,))
        for r in range(PACK):
            squash(1, r)
        for r in range(PACK):
            gather_own(1, r)
            weigh(1, r)
        for r in range(PACK - 1):
            place_scalar(0, r)
        quantise_weights(1)
        drain(vcopy, held, 0, (3,), tag="wq_bf1")
        drain(scopy, carry(1, (1,)), 1, (1,))
        drain(vcopy, carry(1, (0,)), 1, (0,))
        place_vector(0, 3)
        place_vector(1, 0)
        place_scalar(1, 1)
        drain(scopy, carry(1, (2, 3)), 1, (2, 3), tag="sums1_1")

        y = sb("y", [P, PACK, M], F32)
        y_bf = [sb("y_bf%d" % k, [P, OUT_COLS, PACK], BF16) for k in range(M // OUT_COLS)]
        y_codes = sb("y_codes", [P, M], U32)
        y_scale = sb("y_scale", [P, M], U8)
        out_rows = out_0.rearrange("(p r) m -> p r m", r=PACK)
        out_words = out_1[0].rearrange("p c r -> p (c r)").bitcast(I32)

        def add_old(engine, r, cols):
            engine.tensor_tensor(out=y[:, r, cols], in0=old_t[r][:, cols], in1=placed[r][:, cols], op=ALU.add)

        place_scalar(1, 2)
        place_scalar(1, 3)
        add_old(nc.gpsimd, 1, slice(0, POOL_COLS))
        add_old(nc.vector, 1, slice(POOL_COLS, M))
        nc.sync.dma_start(out=out_rows[:, 1, :], in_=y[:, 1, :])
        for r in (0, 2):
            add_old(nc.vector, r, slice(0, M))
            nc.sync.dma_start(out=out_rows[:, r, :], in_=y[:, r, :])
        last = PACK - 1
        for k in range(M // OUT_COLS):
            cols = slice(k * OUT_COLS, (k + 1) * OUT_COLS)
            add_old(nc.vector, last, cols)
        nc.sync.dma_start(out=out_rows[:, last, :], in_=y[:, last, :])

        def round_out(copy, k):
            interleave(copy, y_bf[k][:], y[:, :, k * OUT_COLS : (k + 1) * OUT_COLS])

        def quantise_out(k):
            cols = slice(k * OUT_COLS, (k + 1) * OUT_COLS)
            nc.vector.quantize_mx(
                out=y_codes[:, cols].bitcast(FP8X4), scales=y_scale[:, cols], in_=y_bf[k][:].rearrange("p x r -> p (x r)")
            )

        round_out(scopy, 0)
        round_out(scopy, 3)
        round_out(vcopy, 1)
        round_out(vcopy, 2)
        for pieces in ((0, 1), (2,), (3,)):
            for k in pieces:
                quantise_out(k)
            cols = slice(pieces[0] * OUT_COLS, (pieces[-1] + 1) * OUT_COLS)
            nc.sync.dma_start(out=out_words[:, cols], in_=y_codes[:, cols].bitcast(I32))
        for quad in range(4):
            queue = nc.scalar if quad % 2 else nc.sync
            queue.dma_start(
                out=out_2[0, 4 * quad : 4 * quad + 4, :].bitcast(I32),
                in_=y_scale[32 * quad : 32 * quad + 4, :].bitcast(I32),
            )
